import numpy as np
import ml_dtypes


def mxq(x, axis, fmt="e4m3"):
    dtype, down = {"e4m3": (ml_dtypes.float8_e4m3fn, 7), "e5m2": (ml_dtypes.float8_e5m2, 14)}[fmt]
    v = np.moveaxis(np.asarray(x, np.float32).astype(ml_dtypes.bfloat16).astype(np.float64), axis, -1)
    blocks = v.reshape(v.shape[:-1] + (-1, 32))
    amax = np.abs(blocks).max(-1, keepdims=True)
    byte = np.maximum(np.where(amax > 0, np.frexp(amax)[1] - 1 + 127, 0) - down, 1)
    scale = np.exp2(byte - 127.0)
    codes = (blocks / scale).astype(np.float32).astype(dtype).astype(np.float64)
    return np.moveaxis((codes * scale).reshape(v.shape), -1, axis)


WIDE = False


def mx_kscale(k):
    if not WIDE:
        return np.ones(k)
    levels = np.array([10, -10, 5, -5, 0])
    if k % 512:
        return np.exp2(np.random.permutation(np.resize(levels, k // 32))).repeat(32)
    a = np.empty((k // 512, 16))
    for p in range(k // 512):
        a[p, :8] = np.random.permutation(np.resize(levels, 8))
        for g in range(8):
            far = levels[np.abs(levels - a[p, g]) >= 10]
            a[p, g + 8] = far[np.random.randint(len(far))]
    return np.exp2(a.ravel()).repeat(32)


def f64(x):
    return np.asarray(x).astype(np.float64)


def striped8(idx):
    return np.concatenate([x.reshape(-1, 16).T for x in idx]).astype(np.uint16)


def runs(offs, k):
    lists = np.stack([offs[16 * r : 16 * r + 16].T.reshape(-1) for r in range(8)]).astype(np.int64)
    return lists[np.arange(k) % 512 // 64]


def pack_weight(w):
    k, n = w.shape
    w = f64(np.asarray(w, np.float32).astype(ml_dtypes.bfloat16)).reshape(k // 32, 32, n)
    amax = np.abs(w).max(1)
    byte = np.clip(np.where(amax > 0, np.frexp(amax)[1] - 1 + 127 - 7, 1), 1, 254)
    scaled = (w * np.exp2(127.0 - byte)[:, None, :]).reshape(k, n).astype(np.float32)
    words = np.ascontiguousarray(scaled.reshape(k // 512, 128, 4, n).transpose(0, 1, 3, 2)).astype(ml_dtypes.float8_e4m3fn).view(np.uint8)
    return words, np.ascontiguousarray(byte.astype(np.uint8).reshape(k // 512, 16, n))


def unpack_weight(words, scales):
    g, p, n, _ = words.shape
    vals = np.ascontiguousarray(words).view(ml_dtypes.float8_e4m3fn).astype(np.float64) * np.repeat(np.exp2(scales.astype(np.float64) - 127.0), 8, axis=1)[..., None]
    return vals.transpose(0, 1, 3, 2).reshape(g * 512, n)


K, T, S, H, G, U = 512, 2048, 512, 512, 2048, 1024


def setup_inputs():
    n = np.random.standard_normal
    s = mx_kscale(K)[:, None]
    packed_xT = pack_weight(n((K, T)) * s)
    packed_dT = pack_weight(n((K, G)) / s)
    perm = np.stack([np.random.permutation(U) for _ in range(8)])
    return {
        "x_words": packed_xT[0],
        "x_scales": packed_xT[1],
        "w1": (n((K, H)) / np.sqrt(K) / s).astype(np.float32),
        "gs": (np.random.uniform(0.5, 1.5, (K, 1)) * s).astype(np.float32),
        "d_words": packed_dT[0],
        "d_scales": packed_dT[1],
        "offs": striped8(np.random.randint(0, T, (8, S))),
        "n1": striped8(np.stack([np.random.permutation(S) for _ in range(8)])),
        "n2": striped8(np.stack([np.random.permutation(S) for _ in range(8)])),
        "k1": striped8(np.random.randint(0, G, (8, H))),
        "n3": striped8(perm[:, :S]),
        "n4": striped8(perm[:, S:]),
        "n5": striped8(np.stack([np.random.permutation(S) for _ in range(8)])),
    }


def reference(x_words, x_scales, w1, gs, d_words, d_scales, offs, n1, n2, k1, n3, n4, n5):
    d_k1 = unpack_weight(d_words, d_scales)[np.arange(K)[:, None], runs(k1, K)]
    xq = unpack_weight(x_words, x_scales)[np.arange(K)[:, None], runs(offs, K)]
    y = mxq(f64(w1), 0, "e4m3").T @ xq
    z = f64(gs) * (y - (np.minimum(y[np.arange(H)[:, None], runs(n1, H)], y[np.arange(H)[:, None], runs(n2, H)])))
    h = 0.0625 * ((d_k1.T @ mxq(z, 0, "e4m3")))
    dn = np.minimum(h, h[np.arange(H)[:, None], runs(n5, H)])
    up = np.maximum(h, h[np.arange(H)[:, None], runs(n5, H)])
    ph = np.zeros((H, U))
    ph[np.arange(H)[:, None], runs(n3, H)] = up
    out = ph.copy()
    out[np.arange(H)[:, None], runs(n4, H)] = dn
    return out

@@ -1,0 +1,238 @@
+from contextlib import ExitStack
+
+import concourse.mybir as mybir
+from concourse.masks import make_identity
+
+F32 = mybir.dt.float32
+BF16 = mybir.dt.bfloat16
+I32 = mybir.dt.int32
+U32 = mybir.dt.uint32
+U16 = mybir.dt.uint16
+U8 = mybir.dt.uint8
+FP8X4 = mybir.dt.float8_e4m3fn_x4
+ALU = mybir.AluOpType
+COPY = mybir.ActivationFunctionType.Copy
+RELU = mybir.ActivationFunctionType.Relu
+
+P = 128
+PACK = 4
+K, T, S, H, U = 512, 2048, 512, 512, 1024
+HALF = S // 2
+CHUNKS = [(0, 256), (256, 512)]
+FLOPS = 2 * K * H * S + 2 * H * H * S
+
+
+def tile_picked_hdenseunderpagmx_none_p_kernel(
+    tc, x_words, x_scales, w1, gs, d_words, d_scales, offs, n1, n2, k1, n3, n4, n5, out
+):
+    nc = tc.nc
+    with ExitStack() as ctx:
+        keep = ctx.enter_context(tc.tile_pool(name="keep", bufs=1))
+        psum = ctx.enter_context(tc.psum_pool(name="psum", bufs=1))
+
+        def load_list(name, src):
+            tile = keep.tile([P, S // 16], U16, name=name)
+            nc.sync.dma_start(tile[:], src)
+            return tile
+
+        def load_scale_table(name, src, clear):
+            table = keep.tile([P, T], U8, name=name, tag=name, align_bytes=64)
+            clear.memset(table[:].bitcast(I32), 0)
+            rows = src[0].bitcast(I32)
+            for e in range(2):
+                nc.sync.dma_start(table[:].bitcast(I32)[e:P:16, :], rows[e:16:2, :])
+            return table
+
+        def load_word_table(name, src, tag):
+            table = keep.tile([P, T], I32, name=name, tag=tag, align_bytes=64)
+            nc.sync.dma_start(table[:], src[0].rearrange("p c r -> p (c r)").bitcast(I32))
+            return table
+
+        def place_scale_rows(name, src):
+            plane = keep.tile([P, S], U8, name=name, align_bytes=64)
+            nc.vector.tensor_copy(plane[:].bitcast(I32), src[:].bitcast(I32))
+            for e in range(2):
+                nc.sync.dma_start(plane[:].bitcast(I32)[2 + e : P : 32, :], src[:].bitcast(I32)[16 + e : P : 32, :])
+            return plane
+
+        offs_l = load_list("offs_l", offs)
+        k1_l = load_list("k1_l", k1)
+        n1_l = load_list("n1_l", n1)
+        n2_l = load_list("n2_l", n2)
+        xw_table = load_word_table("xw_table", x_words, "xw_table")
+        n5_l = load_list("n5_l", n5)
+        n3_l = load_list("n3_l", n3)
+        n4_l = load_list("n4_l", n4)
+        xs_table = load_scale_table("xs_table", x_scales, nc.gpsimd)
+        w_rows = w1.rearrange("(p j) c -> p j c", j=PACK)
+        w_raw = []
+        for c in range(2):
+            part = keep.tile([P, PACK, H // 2], F32, name="w_raw%d" % c, tag="w_raw%d" % c, align_bytes=64)
+            nc.sync.dma_start(part[:], w_rows[:, :, c * H // 2 : (c + 1) * H // 2])
+            w_raw.append(part)
+        ds_table = load_scale_table("ds_table", d_scales, nc.vector)
+        gs_sb = keep.tile([P, PACK], F32, name="gs_sb")
+        nc.sync.dma_start(gs_sb[:], gs.rearrange("(p t) o -> p (t o)", t=PACK))
+
+        pages = []
+        for t in range(PACK):
+            page = keep.tile([P, U], F32, name="page%d" % t, align_bytes=64)
+            pages.append(page)
+
+        ident = keep.tile([P, P], F32, name="ident", align_bytes=64)
+        nc.vector.memset(ident[:], 0.0)
+        make_identity(nc, ident[:], nomemset=True)
+
+        xs_picked = keep.tile([P, S], U8, name="xs_picked", align_bytes=64)
+        nc.vector.tensor_copy(xs_picked[:], xs_table[:].indirect(offs_l[:]))
+        xs_plane = place_scale_rows("xs_plane", xs_picked)
+
+        xw_picked = keep.tile([P, S], U32, name="xw_picked", tag="xs_table", align_bytes=64)
+        nc.vector.tensor_copy(xw_picked[:], xw_table[:].bitcast(U32).indirect(offs_l[:]))
+
+        w_bf = keep.tile([P, PACK * H], BF16, name="w_bf", align_bytes=64)
+        w_dst = w_bf[:].rearrange("p (t m j) -> p m j t", t=PACK, j=PACK)
+        for c in range(2):
+            nc.scalar.activation(
+                w_dst[:, c * P // 2 : (c + 1) * P // 2], w_raw[c][:].rearrange("p j (m t) -> p m j t", t=PACK), COPY
+            )
+        dw_table = load_word_table("dw_table", d_words, "w_raw0")
+        w_codes = keep.tile([P, H], U32, name="w_codes", align_bytes=64)
+        w_plane = keep.tile([P, H], U8, name="w_plane", align_bytes=64)
+        for c in range(2):
+            cols = slice(c * H // 2, (c + 1) * H // 2)
+            nc.vector.quantize_mx(
+                out=w_codes[:, cols].bitcast(FP8X4), scales=w_plane[:, cols],
+                in_=w_bf[:, c * PACK * H // 2 : (c + 1) * PACK * H // 2],
+            )
+        ds_picked = keep.tile([P, H], U8, name="ds_picked", align_bytes=64)
+        nc.vector.tensor_copy(ds_picked[:], ds_table[:].indirect(k1_l[:]))
+
+        y_banks = []
+        for t in range(PACK):
+            bank = psum.tile([P, S], F32, name="y_bank%d" % t, tag="early%d" % t)
+            cols = slice(t * P, (t + 1) * P)
+            nc.tensor.matmul_mx(
+                out=bank[:], lhsT=w_codes[:, cols].bitcast(FP8X4), lhsT_scale=w_plane[:, cols],
+                rhs=xw_picked[:].bitcast(FP8X4), rhs_scale=xs_plane[:], start=True, stop=True,
+            )
+            y_banks.append(bank)
+
+        ds_dealt = keep.tile([P, H], U8, name="ds_dealt", align_bytes=64)
+        nc.vector.tensor_copy(
+            ds_dealt[:].rearrange("p (t m) -> p m t", t=PACK), ds_picked[:].rearrange("p (m t) -> p m t", t=PACK)
+        )
+        ds_plane = place_scale_rows("ds_plane", ds_dealt)
+        dw_picked = keep.tile([P, H], U32, name="dw_picked", align_bytes=64)
+        nc.vector.tensor_copy(dw_picked[:], dw_table[:].bitcast(U32).indirect(k1_l[:]))
+        dw_dealt = keep.tile([P, H], U32, name="dw_dealt", align_bytes=64)
+        nc.vector.tensor_copy(
+            dw_dealt[:].bitcast(I32).rearrange("p (t m) -> p m t", t=PACK),
+            dw_picked[:].bitcast(I32).rearrange("p (m t) -> p m t", t=PACK),
+        )
+
+        y_rows = []
+        for t in range(PACK):
+            y_t = keep.tile([P, S], F32, name="y%d" % t, align_bytes=64)
+            if t % 2 == 1:
+                nc.vector.tensor_copy(y_t[:], y_banks[t][:])
+            else:
+                nc.scalar.copy(y_t[:], y_banks[t][:])
+            y_rows.append(y_t)
+
+        h_banks = [psum.tile([P, S], F32, name="h_bank%d" % t) for t in range(PACK)]
+        h_first = keep.tile([P, S], F32, name="h0", align_bytes=64)
+        h_second = keep.tile([P, S], F32, name="h1", align_bytes=64)
+        h_second_neg = keep.tile([P, S], F32, name="h_neg1", tag="neg", align_bytes=64)
+        for c, (lo, hi) in enumerate(CHUNKS):
+            n = hi - lo
+            cols = slice(lo, hi)
+            lcols = slice(lo // 16, hi // 16)
+            gs_b = gs_sb[:].rearrange("p (a t b) -> p a t b", a=1, b=1).to_broadcast([P, n // 2, PACK, 2])
+            first = keep.tile([P, PACK, n], F32, name="first%d" % c, align_bytes=64)
+            second = keep.tile([P, PACK, n], F32, name="second%d" % c, align_bytes=64)
+            low = keep.tile([P, PACK, n], F32, name="low%d" % c, tag="stage%d" % c, align_bytes=64)
+            diff = keep.tile([P, PACK, n], F32, name="diff%d" % c, tag="stage%d" % (c + 1), align_bytes=64)
+            for pair in range(2):
+                for t in (2 * pair, 2 * pair + 1):
+                    nc.scalar.activation(first[:, t, :], y_rows[t][:].indirect(n1_l[:, lcols]), COPY)
+                    if c == 0 and pair == 0:
+                        nc.vector.tensor_copy(second[:, t, :], y_rows[t][:].indirect(n2_l[:, lcols]))
+                    else:
+                        nc.scalar.activation(second[:, t, :], y_rows[t][:].indirect(n2_l[:, lcols]), COPY)
+                both = slice(2 * pair, 2 * pair + 2)
+                nc.vector.tensor_tensor(low[:, both, :], first[:, both, :], second[:, both, :], ALU.min)
+                for t in (2 * pair, 2 * pair + 1):
+                    nc.vector.tensor_tensor(diff[:, t, :], y_rows[t][:, cols], low[:, t, :], ALU.subtract)
+            z_bf = keep.tile([P, PACK * n], BF16, name="z_bf%d" % c, align_bytes=64)
+            nc.vector.tensor_tensor(
+                z_bf[:].rearrange("p (c i t) -> p c t i", i=2, t=PACK),
+                diff[:].rearrange("p t (c i) -> p c t i", i=2),
+                gs_b,
+                ALU.mult,
+            )
+            z_codes = keep.tile([P, n], U32, name="z_codes%d" % c, align_bytes=64)
+            z_plane = keep.tile([P, n], U8, name="z_plane%d" % c, align_bytes=64)
+            nc.vector.quantize_mx(out=z_codes[:].bitcast(FP8X4), scales=z_plane[:], in_=z_bf[:])
+            if c == 1:
+                nc.scalar.activation(h_first[:, 0:lo], h_banks[0][:, 0:lo], COPY, scale=0.0625)
+                nc.scalar.activation(h_second[:, 0:lo], h_banks[1][:, 0:lo], COPY, scale=0.0625)
+                nc.scalar.activation(h_second_neg[:, 0:lo], h_banks[1][:, 0:lo], COPY, scale=-0.0625)
+            for t in range(PACK):
+                rows = slice(t * P, (t + 1) * P)
+                nc.tensor.matmul_mx(
+                    out=h_banks[t][:, cols], lhsT=dw_dealt[:, rows].bitcast(FP8X4), lhsT_scale=ds_plane[:, rows],
+                    rhs=z_codes[:].bitcast(FP8X4), rhs_scale=z_plane[:], start=True, stop=True,
+                )
+
+        out_rows = out.rearrange("(p t) w -> t p w", t=PACK)
+        for t in range(PACK):
+            if t == 0:
+                h_t = h_first
+                nc.vector.tensor_scalar(h_t[:, HALF:S], h_banks[t][:, HALF:S], 0.0625, None, ALU.mult)
+            elif t == 1:
+                h_t = h_second
+                nc.scalar.activation(h_t[:, HALF:S], h_banks[t][:, HALF:S], COPY, scale=0.0625)
+            else:
+                h_t = keep.tile([P, S], F32, name="h%d" % t, tag="hold%d" % t, align_bytes=64)
+                nc.scalar.activation(h_t[:], h_banks[t][:], COPY, scale=0.0625)
+            other = keep.tile([P, S], F32, name="other%d" % t, align_bytes=64)
+            for c in range(2):
+                cols = slice(c * HALF, (c + 1) * HALF)
+                lcols = slice(c * HALF // 16, (c + 1) * HALF // 16)
+                nc.scalar.activation(other[:, cols], h_t[:].indirect(n5_l[:, lcols]), COPY)
+            if t == 0:
+                up = keep.tile([P, S], F32, name="up", align_bytes=64)
+                dn = keep.tile([P, S], F32, name="dn", align_bytes=64)
+                for c in range(2):
+                    cols = slice(c * HALF, (c + 1) * HALF)
+                    lcols = slice(c * HALF // 16, (c + 1) * HALF // 16)
+                    nc.vector.tensor_tensor(up[:, cols], h_t[:, cols], other[:, cols], ALU.max)
+                    nc.vector.tensor_copy(pages[t][:].indirect(n3_l[:, lcols]), up[:, cols])
+                nc.vector.tensor_tensor(dn[:], h_t[:], other[:], ALU.min)
+                nc.vector.tensor_copy(pages[t][:].indirect(n4_l[:]), dn[:])
+            else:
+                if t == 1:
+                    h_neg = h_second_neg
+                    nc.scalar.activation(h_neg[:, HALF:S], h_banks[t][:, HALF:S], COPY, scale=-0.0625)
+                else:
+                    h_neg = keep.tile([P, S], F32, name="h_neg%d" % t, tag="neg", align_bytes=64)
+                    nc.scalar.activation(h_neg[:], h_banks[t][:], COPY, scale=-0.0625)
+                gap_bank = psum.tile([P, S], F32, name="gap_bank%d" % t, tag="early%d" % (2 * (t % 2)))
+                for b in range(S // P):
+                    blk = slice(b * P, (b + 1) * P)
+                    nc.tensor.matmul(gap_bank[:, blk], lhsT=other[:, blk], rhs=ident[:], start=True, stop=False, is_transpose=True)
+                    nc.tensor.matmul(gap_bank[:, blk], lhsT=h_neg[:, blk], rhs=ident[:], start=False, stop=True, is_transpose=True)
+                rise_t = keep.tile([P, S], F32, name="rise_t%d" % t, tag="hold%d" % (t + 1), align_bytes=64)
+                nc.scalar.activation(rise_t[:], gap_bank[:], RELU)
+                rise_bank = psum.tile([P, S], F32, name="rise_bank%d" % t, tag="early%d" % (2 * (t % 2) + 1))
+                for b in range(S // P):
+                    blk = slice(b * P, (b + 1) * P)
+                    nc.tensor.transpose(rise_bank[:, blk], rise_t[:, blk], ident[:])
+                rise = keep.tile([P, S], F32, name="rise%d" % t, align_bytes=64)
+                fall = keep.tile([P, S], F32, name="fall%d" % t, align_bytes=64)
+                nc.scalar.copy(rise[:], rise_bank[:])
+                nc.scalar.activation(fall[:], rise_bank[:], COPY, scale=-1.0)
+                nc.vector.tensor_tensor(pages[t][:].indirect(n3_l[:]), h_t[:], rise[:], ALU.add)
+                nc.vector.tensor_tensor(pages[t][:].indirect(n4_l[:]), other[:], fall[:], ALU.add)
+            nc.sync.dma_start(out_rows[t], pages[t][:])

@@ -19,6 +19,7 @@ PACK = 4
 K, T, S, H, U = 512, 2048, 512, 512, 1024
 HALF = S // 2
 CHUNKS = [(0, 256), (256, 512)]
+HEAD = [(0, 128), (128, 256), (256, 512)]
 FLOPS = 2 * K * H * S + 2 * H * H * S
 
 
@@ -38,9 +39,7 @@ def tile_picked_hdenseunderpagmx_none_p_kernel(
         def load_scale_table(name, src, clear):
             table = keep.tile([P, T], U8, name=name, tag=name, align_bytes=64)
             clear.memset(table[:].bitcast(I32), 0)
-            rows = src[0].bitcast(I32)
-            for e in range(2):
-                nc.sync.dma_start(table[:].bitcast(I32)[e:P:16, :], rows[e:16:2, :])
+            nc.sync.dma_start(table[:].bitcast(I32)[0:P:8, :], src[0].bitcast(I32))
             return table
 
         def load_word_table(name, src, tag):
@@ -48,31 +47,36 @@ def tile_picked_hdenseunderpagmx_none_p_kernel(
             nc.sync.dma_start(table[:], src[0].rearrange("p c r -> p (c r)").bitcast(I32))
             return table
 
-        def place_scale_rows(name, src):
+        def place_scale_rows(name, src, queue):
             plane = keep.tile([P, S], U8, name=name, align_bytes=64)
             nc.vector.tensor_copy(plane[:].bitcast(I32), src[:].bitcast(I32))
-            for e in range(2):
-                nc.sync.dma_start(plane[:].bitcast(I32)[2 + e : P : 32, :], src[:].bitcast(I32)[16 + e : P : 32, :])
+            for j in range(1, 4):
+                queue.dma_start(plane[:].bitcast(I32)[j:P:32, :], src[:].bitcast(I32)[8 * j : P : 32, :])
             return plane
 
+        w_rows = w1.rearrange("(p j) c -> p j c", j=PACK)
+
+        def load_w_half(c):
+            part = keep.tile([P, PACK, H // 2], F32, name="w_raw%d" % c, tag="w_raw%d" % c, align_bytes=64)
+            nc.sync.dma_start(part[:], w_rows[:, :, c * H // 2 : (c + 1) * H // 2])
+            return part
+
         offs_l = load_list("offs_l", offs)
+        w_raw = [load_w_half(0)]
         k1_l = load_list("k1_l", k1)
         n1_l = load_list("n1_l", n1)
+        xs_table = load_scale_table("xs_table", x_scales, nc.vector)
         n2_l = load_list("n2_l", n2)
+        ds_table = load_scale_table("ds_table", d_scales, nc.vector)
+        w_raw.append(load_w_half(1))
         xw_table = load_word_table("xw_table", x_words, "xw_table")
         n5_l = load_list("n5_l", n5)
         n3_l = load_list("n3_l", n3)
         n4_l = load_list("n4_l", n4)
-        xs_table = load_scale_table("xs_table", x_scales, nc.gpsimd)
-        w_rows = w1.rearrange("(p j) c -> p j c", j=PACK)
-        w_raw = []
-        for c in range(2):
-            part = keep.tile([P, PACK, H // 2], F32, name="w_raw%d" % c, tag="w_raw%d" % c, align_bytes=64)
-            nc.sync.dma_start(part[:], w_rows[:, :, c * H // 2 : (c + 1) * H // 2])
-            w_raw.append(part)
-        ds_table = load_scale_table("ds_table", d_scales, nc.vector)
         gs_sb = keep.tile([P, PACK], F32, name="gs_sb")
-        nc.sync.dma_start(gs_sb[:], gs.rearrange("(p t) o -> p (t o)", t=PACK))
+        nc.gpsimd.dma_start(gs_sb[:], gs.rearrange("(p t) o -> p (t o)", t=PACK))
+        gs_neg = keep.tile([P, PACK], F32, name="gs_neg")
+        nc.gpsimd.tensor_scalar(gs_neg[:], gs_sb[:], -1.0, 0.0, ALU.mult, ALU.add)
 
         pages = []
         for t in range(PACK):
@@ -80,15 +84,11 @@ def tile_picked_hdenseunderpagmx_none_p_kernel(
             pages.append(page)
 
         ident = keep.tile([P, P], F32, name="ident", align_bytes=64)
-        nc.vector.memset(ident[:], 0.0)
-        make_identity(nc, ident[:], nomemset=True)
+        make_identity(nc, ident[:])
 
         xs_picked = keep.tile([P, S], U8, name="xs_picked", align_bytes=64)
         nc.vector.tensor_copy(xs_picked[:], xs_table[:].indirect(offs_l[:]))
-        xs_plane = place_scale_rows("xs_plane", xs_picked)
-
-        xw_picked = keep.tile([P, S], U32, name="xw_picked", tag="xs_table", align_bytes=64)
-        nc.vector.tensor_copy(xw_picked[:], xw_table[:].bitcast(U32).indirect(offs_l[:]))
+        xs_plane = place_scale_rows("xs_plane", xs_picked, nc.sync)
 
         w_bf = keep.tile([P, PACK * H], BF16, name="w_bf", align_bytes=64)
         w_dst = w_bf[:].rearrange("p (t m j) -> p m j t", t=PACK, j=PACK)
@@ -96,7 +96,7 @@ def tile_picked_hdenseunderpagmx_none_p_kernel(
             nc.scalar.activation(
                 w_dst[:, c * P // 2 : (c + 1) * P // 2], w_raw[c][:].rearrange("p j (m t) -> p m j t", t=PACK), COPY
             )
-        dw_table = load_word_table("dw_table", d_words, "w_raw0")
+        dw_table = load_word_table("dw_table", d_words, "w_raw1")
         w_codes = keep.tile([P, H], U32, name="w_codes", align_bytes=64)
         w_plane = keep.tile([P, H], U8, name="w_plane", align_bytes=64)
         for c in range(2):
@@ -105,6 +105,8 @@ def tile_picked_hdenseunderpagmx_none_p_kernel(
                 out=w_codes[:, cols].bitcast(FP8X4), scales=w_plane[:, cols],
                 in_=w_bf[:, c * PACK * H // 2 : (c + 1) * PACK * H // 2],
             )
+        xw_picked = keep.tile([P, S], U32, name="xw_picked", align_bytes=64)
+        nc.vector.tensor_copy(xw_picked[:], xw_table[:].bitcast(U32).indirect(offs_l[:]))
         ds_picked = keep.tile([P, H], U8, name="ds_picked", align_bytes=64)
         nc.vector.tensor_copy(ds_picked[:], ds_table[:].indirect(k1_l[:]))
 
@@ -122,7 +124,10 @@ def tile_picked_hdenseunderpagmx_none_p_kernel(
         nc.vector.tensor_copy(
             ds_dealt[:].rearrange("p (t m) -> p m t", t=PACK), ds_picked[:].rearrange("p (m t) -> p m t", t=PACK)
         )
-        ds_plane = place_scale_rows("ds_plane", ds_dealt)
+        ds_plane = keep.tile([P, H], U8, name="ds_plane", align_bytes=64)
+        nc.gpsimd.memset(ds_plane[:].bitcast(I32), 0)
+        for j in range(4):
+            nc.gpsimd.dma_start(ds_plane[:].bitcast(I32)[j:P:32, :], ds_dealt[:].bitcast(I32)[8 * j : P : 32, :])
         dw_picked = keep.tile([P, H], U32, name="dw_picked", align_bytes=64)
         nc.vector.tensor_copy(dw_picked[:], dw_table[:].bitcast(U32).indirect(k1_l[:]))
         dw_dealt = keep.tile([P, H], U32, name="dw_dealt", align_bytes=64)
@@ -132,47 +137,60 @@ def tile_picked_hdenseunderpagmx_none_p_kernel(
         )
 
         y_rows = []
+        y_weighted = []
         for t in range(PACK):
             y_t = keep.tile([P, S], F32, name="y%d" % t, align_bytes=64)
-            if t % 2 == 1:
+            if t > 0:
                 nc.vector.tensor_copy(y_t[:], y_banks[t][:])
             else:
                 nc.scalar.copy(y_t[:], y_banks[t][:])
             y_rows.append(y_t)
+            y_w = keep.tile([P, S], F32, name="y_weighted%d" % t, align_bytes=64)
+            nc.gpsimd.tensor_scalar(y_w[:], y_t[:], gs_sb[:, t : t + 1], 0.0, ALU.mult, ALU.add)
+            y_weighted.append(y_w)
 
         h_banks = [psum.tile([P, S], F32, name="h_bank%d" % t) for t in range(PACK)]
         h_first = keep.tile([P, S], F32, name="h0", align_bytes=64)
         h_second = keep.tile([P, S], F32, name="h1", align_bytes=64)
-        h_second_neg = keep.tile([P, S], F32, name="h_neg1", tag="neg", align_bytes=64)
-        for c, (lo, hi) in enumerate(CHUNKS):
-            n = hi - lo
-            cols = slice(lo, hi)
+        h_second_neg = keep.tile([P, S], F32, name="h_neg1", tag="hold2", align_bytes=64)
+        z_rows = keep.tile([P, 2, PACK, HALF], BF16, name="z_rows", align_bytes=64)
+
+        def fetch(t, lo, hi, first, second):
             lcols = slice(lo // 16, hi // 16)
-            gs_b = gs_sb[:].rearrange("p (a t b) -> p a t b", a=1, b=1).to_broadcast([P, n // 2, PACK, 2])
-            first = keep.tile([P, PACK, n], F32, name="first%d" % c, align_bytes=64)
-            second = keep.tile([P, PACK, n], F32, name="second%d" % c, align_bytes=64)
-            low = keep.tile([P, PACK, n], F32, name="low%d" % c, tag="stage%d" % c, align_bytes=64)
-            diff = keep.tile([P, PACK, n], F32, name="diff%d" % c, tag="stage%d" % (c + 1), align_bytes=64)
-            for pair in range(2):
-                for t in (2 * pair, 2 * pair + 1):
-                    nc.scalar.activation(first[:, t, :], y_rows[t][:].indirect(n1_l[:, lcols]), COPY)
-                    if c == 0 and pair == 0:
-                        nc.vector.tensor_copy(second[:, t, :], y_rows[t][:].indirect(n2_l[:, lcols]))
-                    else:
-                        nc.scalar.activation(second[:, t, :], y_rows[t][:].indirect(n2_l[:, lcols]), COPY)
-                both = slice(2 * pair, 2 * pair + 2)
-                nc.vector.tensor_tensor(low[:, both, :], first[:, both, :], second[:, both, :], ALU.min)
-                for t in (2 * pair, 2 * pair + 1):
-                    nc.vector.tensor_tensor(diff[:, t, :], y_rows[t][:, cols], low[:, t, :], ALU.subtract)
-            z_bf = keep.tile([P, PACK * n], BF16, name="z_bf%d" % c, align_bytes=64)
-            nc.vector.tensor_tensor(
-                z_bf[:].rearrange("p (c i t) -> p c t i", i=2, t=PACK),
-                diff[:].rearrange("p t (c i) -> p c t i", i=2),
-                gs_b,
-                ALU.mult,
+            nc.scalar.activation(first, y_rows[t][:].indirect(n1_l[:, lcols]), COPY)
+            if t == 0:
+                nc.vector.tensor_copy(second, y_rows[t][:].indirect(n2_l[:, lcols]))
+            else:
+                nc.scalar.activation(second, y_rows[t][:].indirect(n2_l[:, lcols]), COPY)
+
+        for t in range(2):
+            first = keep.tile([P, S], F32, name="first%d" % t, align_bytes=64)
+            second = keep.tile([P, S], F32, name="second%d" % t, align_bytes=64)
+            low = keep.tile([P, S], F32, name="low%d" % t, align_bytes=64)
+            for lo, hi in CHUNKS:
+                fetch(t, lo, hi, first[:, lo:hi], second[:, lo:hi])
+            nc.vector.tensor_tensor(low[:], first[:], second[:], ALU.min)
+            nc.vector.scalar_tensor_tensor(
+                z_rows[:, :, t, :], low[:].rearrange("p (c n) -> p c n", c=2), gs_neg[:, t : t + 1],
+                y_weighted[t][:].rearrange("p (c n) -> p c n", c=2), ALU.mult, ALU.add,
             )
-            z_codes = keep.tile([P, n], U32, name="z_codes%d" % c, align_bytes=64)
-            z_plane = keep.tile([P, n], U8, name="z_plane%d" % c, align_bytes=64)
+        for c, (lo, hi) in enumerate(CHUNKS):
+            cols = slice(lo, hi)
+            for t in range(2, PACK):
+                first = keep.tile([P, HALF], F32, name="first%d_%d" % (t, c), align_bytes=64)
+                second = keep.tile([P, HALF], F32, name="second%d_%d" % (t, c), align_bytes=64)
+                low = keep.tile([P, HALF], F32, name="low%d_%d" % (t, c), tag="stage%d_%d" % (c, t), align_bytes=64)
+                fetch(t, lo, hi, first[:], second[:])
+                nc.vector.tensor_tensor(low[:], first[:], second[:], ALU.min)
+                nc.vector.scalar_tensor_tensor(
+                    z_rows[:, c, t, :], low[:], gs_neg[:, t : t + 1], y_weighted[t][:, cols], ALU.mult, ALU.add
+                )
+            z_bf = keep.tile([P, PACK * HALF], BF16, name="z_bf%d" % c, tag="stage%d_3" % (c + 1), align_bytes=64)
+            nc.vector.tensor_copy(
+                z_bf[:].rearrange("p (c i t) -> p c t i", i=4, t=PACK), z_rows[:, c].rearrange("p t (c i) -> p c t i", i=4)
+            )
+            z_codes = keep.tile([P, HALF], U32, name="z_codes%d" % c, align_bytes=64)
+            z_plane = keep.tile([P, HALF], U8, name="z_plane%d" % c, align_bytes=64)
             nc.vector.quantize_mx(out=z_codes[:].bitcast(FP8X4), scales=z_plane[:], in_=z_bf[:])
             if c == 1:
                 nc.scalar.activation(h_first[:, 0:lo], h_banks[0][:, 0:lo], COPY, scale=0.0625)
@@ -194,36 +212,36 @@ def tile_picked_hdenseunderpagmx_none_p_kernel(
                 h_t = h_second
                 nc.scalar.activation(h_t[:, HALF:S], h_banks[t][:, HALF:S], COPY, scale=0.0625)
             else:
-                h_t = keep.tile([P, S], F32, name="h%d" % t, tag="hold%d" % t, align_bytes=64)
+                h_t = keep.tile([P, S], F32, name="h%d" % t, tag="hold2" if t == 2 else "turned2", align_bytes=64)
                 nc.scalar.activation(h_t[:], h_banks[t][:], COPY, scale=0.0625)
             other = keep.tile([P, S], F32, name="other%d" % t, align_bytes=64)
-            for c in range(2):
-                cols = slice(c * HALF, (c + 1) * HALF)
-                lcols = slice(c * HALF // 16, (c + 1) * HALF // 16)
+            for lo, hi in HEAD if t == 0 else CHUNKS:
+                cols = slice(lo, hi)
+                lcols = slice(lo // 16, hi // 16)
                 nc.scalar.activation(other[:, cols], h_t[:].indirect(n5_l[:, lcols]), COPY)
             if t == 0:
                 up = keep.tile([P, S], F32, name="up", align_bytes=64)
                 dn = keep.tile([P, S], F32, name="dn", align_bytes=64)
-                for c in range(2):
-                    cols = slice(c * HALF, (c + 1) * HALF)
-                    lcols = slice(c * HALF // 16, (c + 1) * HALF // 16)
-                    nc.vector.tensor_tensor(up[:, cols], h_t[:, cols], other[:, cols], ALU.max)
-                    nc.vector.tensor_copy(pages[t][:].indirect(n3_l[:, lcols]), up[:, cols])
+                lead = HEAD[0][1]
+                nc.vector.tensor_tensor(up[:, 0:lead], h_t[:, 0:lead], other[:, 0:lead], ALU.max)
+                nc.vector.tensor_copy(pages[t][:].indirect(n3_l[:, 0 : lead // 16]), up[:, 0:lead])
+                nc.vector.tensor_tensor(up[:, lead:S], h_t[:, lead:S], other[:, lead:S], ALU.max)
                 nc.vector.tensor_tensor(dn[:], h_t[:], other[:], ALU.min)
+                nc.vector.tensor_copy(pages[t][:].indirect(n3_l[:, lead // 16 : S // 16]), up[:, lead:S])
                 nc.vector.tensor_copy(pages[t][:].indirect(n4_l[:]), dn[:])
             else:
                 if t == 1:
                     h_neg = h_second_neg
                     nc.scalar.activation(h_neg[:, HALF:S], h_banks[t][:, HALF:S], COPY, scale=-0.0625)
                 else:
-                    h_neg = keep.tile([P, S], F32, name="h_neg%d" % t, tag="neg", align_bytes=64)
+                    h_neg = keep.tile([P, S], F32, name="h_neg%d" % t, tag="turned%d" % t, align_bytes=64)
                     nc.scalar.activation(h_neg[:], h_banks[t][:], COPY, scale=-0.0625)
                 gap_bank = psum.tile([P, S], F32, name="gap_bank%d" % t, tag="early%d" % (2 * (t % 2)))
                 for b in range(S // P):
                     blk = slice(b * P, (b + 1) * P)
                     nc.tensor.matmul(gap_bank[:, blk], lhsT=other[:, blk], rhs=ident[:], start=True, stop=False, is_transpose=True)
                     nc.tensor.matmul(gap_bank[:, blk], lhsT=h_neg[:, blk], rhs=ident[:], start=False, stop=True, is_transpose=True)
-                rise_t = keep.tile([P, S], F32, name="rise_t%d" % t, tag="hold%d" % (t + 1), align_bytes=64)
+                rise_t = keep.tile([P, S], F32, name="rise_t%d" % t, tag="turned%d" % (t + 1), align_bytes=64)
                 nc.scalar.activation(rise_t[:], gap_bank[:], RELU)
                 rise_bank = psum.tile([P, S], F32, name="rise_bank%d" % t, tag="early%d" % (2 * (t % 2) + 1))
                 for b in range(S // P):

@@ -106,23 +106,23 @@ def tile_picked_hdenseunderpagmx_none_p_kernel(
                 in_=w_bf[:, c * PACK * H // 2 : (c + 1) * PACK * H // 2],
             )
         xw_picked = keep.tile([P, S], U32, name="xw_picked", align_bytes=64)
-        nc.vector.tensor_copy(xw_picked[:], xw_table[:].bitcast(U32).indirect(offs_l[:]))
+        for lo, hi in CHUNKS:
+            nc.vector.tensor_copy(xw_picked[:, lo:hi], xw_table[:].bitcast(U32).indirect(offs_l[:, lo // 16 : hi // 16]))
         ds_picked = keep.tile([P, H], U8, name="ds_picked", align_bytes=64)
         nc.vector.tensor_copy(ds_picked[:], ds_table[:].indirect(k1_l[:]))
 
-        y_banks = []
-        for t in range(PACK):
-            bank = psum.tile([P, S], F32, name="y_bank%d" % t, tag="early%d" % t)
-            cols = slice(t * P, (t + 1) * P)
-            nc.tensor.matmul_mx(
-                out=bank[:], lhsT=w_codes[:, cols].bitcast(FP8X4), lhsT_scale=w_plane[:, cols],
-                rhs=xw_picked[:].bitcast(FP8X4), rhs_scale=xs_plane[:], start=True, stop=True,
-            )
-            y_banks.append(bank)
+        y_banks = [psum.tile([P, S], F32, name="y_bank%d" % t, tag="early%d" % t) for t in range(PACK)]
+        for lo, hi in CHUNKS:
+            for t in range(PACK):
+                rows = slice(t * P, (t + 1) * P)
+                nc.tensor.matmul_mx(
+                    out=y_banks[t][:, lo:hi], lhsT=w_codes[:, rows].bitcast(FP8X4), lhsT_scale=w_plane[:, rows],
+                    rhs=xw_picked[:, lo:hi].bitcast(FP8X4), rhs_scale=xs_plane[:, lo:hi], start=True, stop=True,
+                )
 
         ds_dealt = keep.tile([P, H], U8, name="ds_dealt", align_bytes=64)
         nc.vector.tensor_copy(
-            ds_dealt[:].rearrange("p (t m) -> p m t", t=PACK), ds_picked[:].rearrange("p (m t) -> p m t", t=PACK)
+            ds_dealt[:].rearrange("p (t m) -> p t m", t=PACK), ds_picked[:].rearrange("p (m t) -> p t m", t=PACK)
         )
         ds_plane = keep.tile([P, H], U8, name="ds_plane", align_bytes=64)
         nc.gpsimd.memset(ds_plane[:].bitcast(I32), 0)
@@ -132,8 +132,8 @@ def tile_picked_hdenseunderpagmx_none_p_kernel(
         nc.vector.tensor_copy(dw_picked[:], dw_table[:].bitcast(U32).indirect(k1_l[:]))
         dw_dealt = keep.tile([P, H], U32, name="dw_dealt", align_bytes=64)
         nc.vector.tensor_copy(
-            dw_dealt[:].bitcast(I32).rearrange("p (t m) -> p m t", t=PACK),
-            dw_picked[:].bitcast(I32).rearrange("p (m t) -> p m t", t=PACK),
+            dw_dealt[:].bitcast(I32).rearrange("p (t m i) -> p m t i", t=PACK, i=4),
+            dw_picked[:].bitcast(I32).rearrange("p (m i t) -> p m t i", t=PACK, i=4),
         )
 
         y_rows = []

from contextlib import ExitStack

import concourse.mybir as mybir
from concourse.masks import make_identity

F32 = mybir.dt.float32
BF16 = mybir.dt.bfloat16
I32 = mybir.dt.int32
U32 = mybir.dt.uint32
U16 = mybir.dt.uint16
U8 = mybir.dt.uint8
FP8X4 = mybir.dt.float8_e4m3fn_x4
ALU = mybir.AluOpType
COPY = mybir.ActivationFunctionType.Copy
RELU = mybir.ActivationFunctionType.Relu

P = 128
PACK = 4
K, T, S, H, U = 512, 2048, 512, 512, 1024
HALF = S // 2
CHUNKS = [(0, 256), (256, 512)]
HEAD = [(0, 128), (128, 256), (256, 512)]
FLOPS = 2 * K * H * S + 2 * H * H * S


def tile_picked_hdenseunderpagmx_none_p_kernel(
    tc, x_words, x_scales, w1, gs, d_words, d_scales, offs, n1, n2, k1, n3, n4, n5, out
):
    nc = tc.nc
    with ExitStack() as ctx:
        keep = ctx.enter_context(tc.tile_pool(name="keep", bufs=1))
        psum = ctx.enter_context(tc.psum_pool(name="psum", bufs=1))

        def load_list(name, src):
            tile = keep.tile([P, S // 16], U16, name=name)
            nc.sync.dma_start(tile[:], src)
            return tile

        def load_scale_table(name, src, clear):
            table = keep.tile([P, T], U8, name=name, tag=name, align_bytes=64)
            clear.memset(table[:].bitcast(I32), 0)
            nc.sync.dma_start(table[:].bitcast(I32)[0:P:8, :], src[0].bitcast(I32))
            return table

        def load_word_table(name, src, tag):
            table = keep.tile([P, T], I32, name=name, tag=tag, align_bytes=64)
            nc.sync.dma_start(table[:], src[0].rearrange("p c r -> p (c r)").bitcast(I32))
            return table

        def place_scale_rows(name, src, queue):
            plane = keep.tile([P, S], U8, name=name, align_bytes=64)
            nc.vector.tensor_copy(plane[:].bitcast(I32), src[:].bitcast(I32))
            for j in range(1, 4):
                queue.dma_start(plane[:].bitcast(I32)[j:P:32, :], src[:].bitcast(I32)[8 * j : P : 32, :])
            return plane

        w_rows = w1.rearrange("(p j) c -> p j c", j=PACK)

        def load_w_half(c):
            part = keep.tile([P, PACK, H // 2], F32, name="w_raw%d" % c, tag="w_raw%d" % c, align_bytes=64)
            nc.sync.dma_start(part[:], w_rows[:, :, c * H // 2 : (c + 1) * H // 2])
            return part

        offs_l = load_list("offs_l", offs)
        w_raw = [load_w_half(0)]
        k1_l = load_list("k1_l", k1)
        n1_l = load_list("n1_l", n1)
        xs_table = load_scale_table("xs_table", x_scales, nc.vector)
        n2_l = load_list("n2_l", n2)
        ds_table = load_scale_table("ds_table", d_scales, nc.vector)
        w_raw.append(load_w_half(1))
        xw_table = load_word_table("xw_table", x_words, "xw_table")
        n5_l = load_list("n5_l", n5)
        n3_l = load_list("n3_l", n3)
        n4_l = load_list("n4_l", n4)
        gs_sb = keep.tile([P, PACK], F32, name="gs_sb")
        nc.gpsimd.dma_start(gs_sb[:], gs.rearrange("(p t) o -> p (t o)", t=PACK))
        gs_neg = keep.tile([P, PACK], F32, name="gs_neg")
        nc.gpsimd.tensor_scalar(gs_neg[:], gs_sb[:], -1.0, 0.0, ALU.mult, ALU.add)

        pages = []
        for t in range(PACK):
            page = keep.tile([P, U], F32, name="page%d" % t, align_bytes=64)
            pages.append(page)

        ident = keep.tile([P, P], F32, name="ident", align_bytes=64)
        make_identity(nc, ident[:])

        xs_picked = keep.tile([P, S], U8, name="xs_picked", align_bytes=64)
        nc.vector.tensor_copy(xs_picked[:], xs_table[:].indirect(offs_l[:]))
        xs_plane = place_scale_rows("xs_plane", xs_picked, nc.sync)

        w_bf = keep.tile([P, PACK * H], BF16, name="w_bf", align_bytes=64)
        w_dst = w_bf[:].rearrange("p (t m j) -> p m j t", t=PACK, j=PACK)
        for c in range(2):
            nc.scalar.activation(
                w_dst[:, c * P // 2 : (c + 1) * P // 2], w_raw[c][:].rearrange("p j (m t) -> p m j t", t=PACK), COPY
            )
        dw_table = load_word_table("dw_table", d_words, "w_raw1")
        w_codes = keep.tile([P, H], U32, name="w_codes", align_bytes=64)
        w_plane = keep.tile([P, H], U8, name="w_plane", align_bytes=64)
        for c in range(2):
            cols = slice(c * H // 2, (c + 1) * H // 2)
            nc.vector.quantize_mx(
                out=w_codes[:, cols].bitcast(FP8X4), scales=w_plane[:, cols],
                in_=w_bf[:, c * PACK * H // 2 : (c + 1) * PACK * H // 2],
            )
        xw_picked = keep.tile([P, S], U32, name="xw_picked", align_bytes=64)
        for lo, hi in CHUNKS:
            nc.vector.tensor_copy(xw_picked[:, lo:hi], xw_table[:].bitcast(U32).indirect(offs_l[:, lo // 16 : hi // 16]))
        ds_picked = keep.tile([P, H], U8, name="ds_picked", align_bytes=64)
        nc.vector.tensor_copy(ds_picked[:], ds_table[:].indirect(k1_l[:]))

        y_banks = [psum.tile([P, S], F32, name="y_bank%d" % t, tag="early%d" % t) for t in range(PACK)]
        for lo, hi in CHUNKS:
            for t in range(PACK):
                rows = slice(t * P, (t + 1) * P)
                nc.tensor.matmul_mx(
                    out=y_banks[t][:, lo:hi], lhsT=w_codes[:, rows].bitcast(FP8X4), lhsT_scale=w_plane[:, rows],
                    rhs=xw_picked[:, lo:hi].bitcast(FP8X4), rhs_scale=xs_plane[:, lo:hi], start=True, stop=True,
                )

        ds_dealt = keep.tile([P, H], U8, name="ds_dealt", align_bytes=64)
        nc.vector.tensor_copy(
            ds_dealt[:].rearrange("p (t m) -> p t m", t=PACK), ds_picked[:].rearrange("p (m t) -> p t m", t=PACK)
        )
        ds_plane = keep.tile([P, H], U8, name="ds_plane", align_bytes=64)
        nc.gpsimd.memset(ds_plane[:].bitcast(I32), 0)
        for j in range(4):
            nc.gpsimd.dma_start(ds_plane[:].bitcast(I32)[j:P:32, :], ds_dealt[:].bitcast(I32)[8 * j : P : 32, :])
        dw_picked = keep.tile([P, H], U32, name="dw_picked", align_bytes=64)
        nc.vector.tensor_copy(dw_picked[:], dw_table[:].bitcast(U32).indirect(k1_l[:]))
        dw_dealt = keep.tile([P, H], U32, name="dw_dealt", align_bytes=64)
        nc.vector.tensor_copy(
            dw_dealt[:].bitcast(I32).rearrange("p (t m i) -> p m t i", t=PACK, i=4),
            dw_picked[:].bitcast(I32).rearrange("p (m i t) -> p m t i", t=PACK, i=4),
        )

        y_rows = []
        y_weighted = []
        for t in range(PACK):
            y_t = keep.tile([P, S], F32, name="y%d" % t, align_bytes=64)
            if t > 0:
                nc.vector.tensor_copy(y_t[:], y_banks[t][:])
            else:
                nc.scalar.copy(y_t[:], y_banks[t][:])
            y_rows.append(y_t)
            y_w = keep.tile([P, S], F32, name="y_weighted%d" % t, align_bytes=64)
            nc.gpsimd.tensor_scalar(y_w[:], y_t[:], gs_sb[:, t : t + 1], 0.0, ALU.mult, ALU.add)
            y_weighted.append(y_w)

        h_banks = [psum.tile([P, S], F32, name="h_bank%d" % t) for t in range(PACK)]
        h_first = keep.tile([P, S], F32, name="h0", align_bytes=64)
        h_second = keep.tile([P, S], F32, name="h1", align_bytes=64)
        h_second_neg = keep.tile([P, S], F32, name="h_neg1", tag="hold2", align_bytes=64)
        z_rows = keep.tile([P, 2, PACK, HALF], BF16, name="z_rows", align_bytes=64)

        def fetch(t, lo, hi, first, second):
            lcols = slice(lo // 16, hi // 16)
            nc.scalar.activation(first, y_rows[t][:].indirect(n1_l[:, lcols]), COPY)
            if t == 0:
                nc.vector.tensor_copy(second, y_rows[t][:].indirect(n2_l[:, lcols]))
            else:
                nc.scalar.activation(second, y_rows[t][:].indirect(n2_l[:, lcols]), COPY)

        for t in range(2):
            first = keep.tile([P, S], F32, name="first%d" % t, align_bytes=64)
            second = keep.tile([P, S], F32, name="second%d" % t, align_bytes=64)
            low = keep.tile([P, S], F32, name="low%d" % t, align_bytes=64)
            for lo, hi in CHUNKS:
                fetch(t, lo, hi, first[:, lo:hi], second[:, lo:hi])
            nc.vector.tensor_tensor(low[:], first[:], second[:], ALU.min)
            nc.vector.scalar_tensor_tensor(
                z_rows[:, :, t, :], low[:].rearrange("p (c n) -> p c n", c=2), gs_neg[:, t : t + 1],
                y_weighted[t][:].rearrange("p (c n) -> p c n", c=2), ALU.mult, ALU.add,
            )
        for c, (lo, hi) in enumerate(CHUNKS):
            cols = slice(lo, hi)
            for t in range(2, PACK):
                first = keep.tile([P, HALF], F32, name="first%d_%d" % (t, c), align_bytes=64)
                second = keep.tile([P, HALF], F32, name="second%d_%d" % (t, c), align_bytes=64)
                low = keep.tile([P, HALF], F32, name="low%d_%d" % (t, c), tag="stage%d_%d" % (c, t), align_bytes=64)
                fetch(t, lo, hi, first[:], second[:])
                nc.vector.tensor_tensor(low[:], first[:], second[:], ALU.min)
                nc.vector.scalar_tensor_tensor(
                    z_rows[:, c, t, :], low[:], gs_neg[:, t : t + 1], y_weighted[t][:, cols], ALU.mult, ALU.add
                )
            z_bf = keep.tile([P, PACK * HALF], BF16, name="z_bf%d" % c, tag="stage%d_3" % (c + 1), align_bytes=64)
            nc.vector.tensor_copy(
                z_bf[:].rearrange("p (c i t) -> p c t i", i=4, t=PACK), z_rows[:, c].rearrange("p t (c i) -> p c t i", i=4)
            )
            z_codes = keep.tile([P, HALF], U32, name="z_codes%d" % c, align_bytes=64)
            z_plane = keep.tile([P, HALF], U8, name="z_plane%d" % c, align_bytes=64)
            nc.vector.quantize_mx(out=z_codes[:].bitcast(FP8X4), scales=z_plane[:], in_=z_bf[:])
            if c == 1:
                nc.scalar.activation(h_first[:, 0:lo], h_banks[0][:, 0:lo], COPY, scale=0.0625)
                nc.scalar.activation(h_second[:, 0:lo], h_banks[1][:, 0:lo], COPY, scale=0.0625)
                nc.scalar.activation(h_second_neg[:, 0:lo], h_banks[1][:, 0:lo], COPY, scale=-0.0625)
            for t in range(PACK):
                rows = slice(t * P, (t + 1) * P)
                nc.tensor.matmul_mx(
                    out=h_banks[t][:, cols], lhsT=dw_dealt[:, rows].bitcast(FP8X4), lhsT_scale=ds_plane[:, rows],
                    rhs=z_codes[:].bitcast(FP8X4), rhs_scale=z_plane[:], start=True, stop=True,
                )

        out_rows = out.rearrange("(p t) w -> t p w", t=PACK)
        for t in range(PACK):
            if t == 0:
                h_t = h_first
                nc.vector.tensor_scalar(h_t[:, HALF:S], h_banks[t][:, HALF:S], 0.0625, None, ALU.mult)
            elif t == 1:
                h_t = h_second
                nc.scalar.activation(h_t[:, HALF:S], h_banks[t][:, HALF:S], COPY, scale=0.0625)
            else:
                h_t = keep.tile([P, S], F32, name="h%d" % t, tag="hold2" if t == 2 else "turned2", align_bytes=64)
                nc.scalar.activation(h_t[:], h_banks[t][:], COPY, scale=0.0625)
            other = keep.tile([P, S], F32, name="other%d" % t, align_bytes=64)
            for lo, hi in HEAD if t == 0 else CHUNKS:
                cols = slice(lo, hi)
                lcols = slice(lo // 16, hi // 16)
                nc.scalar.activation(other[:, cols], h_t[:].indirect(n5_l[:, lcols]), COPY)
            if t == 0:
                up = keep.tile([P, S], F32, name="up", align_bytes=64)
                dn = keep.tile([P, S], F32, name="dn", align_bytes=64)
                lead = HEAD[0][1]
                nc.vector.tensor_tensor(up[:, 0:lead], h_t[:, 0:lead], other[:, 0:lead], ALU.max)
                nc.vector.tensor_copy(pages[t][:].indirect(n3_l[:, 0 : lead // 16]), up[:, 0:lead])
                nc.vector.tensor_tensor(up[:, lead:S], h_t[:, lead:S], other[:, lead:S], ALU.max)
                nc.vector.tensor_tensor(dn[:], h_t[:], other[:], ALU.min)
                nc.vector.tensor_copy(pages[t][:].indirect(n3_l[:, lead // 16 : S // 16]), up[:, lead:S])
                nc.vector.tensor_copy(pages[t][:].indirect(n4_l[:]), dn[:])
            else:
                if t == 1:
                    h_neg = h_second_neg
                    nc.scalar.activation(h_neg[:, HALF:S], h_banks[t][:, HALF:S], COPY, scale=-0.0625)
                else:
                    h_neg = keep.tile([P, S], F32, name="h_neg%d" % t, tag="turned%d" % t, align_bytes=64)
                    nc.scalar.activation(h_neg[:], h_banks[t][:], COPY, scale=-0.0625)
                gap_bank = psum.tile([P, S], F32, name="gap_bank%d" % t, tag="early%d" % (2 * (t % 2)))
                for b in range(S // P):
                    blk = slice(b * P, (b + 1) * P)
                    nc.tensor.matmul(gap_bank[:, blk], lhsT=other[:, blk], rhs=ident[:], start=True, stop=False, is_transpose=True)
                    nc.tensor.matmul(gap_bank[:, blk], lhsT=h_neg[:, blk], rhs=ident[:], start=False, stop=True, is_transpose=True)
                rise_t = keep.tile([P, S], F32, name="rise_t%d" % t, tag="turned%d" % (t + 1), align_bytes=64)
                nc.scalar.activation(rise_t[:], gap_bank[:], RELU)
                rise_bank = psum.tile([P, S], F32, name="rise_bank%d" % t, tag="early%d" % (2 * (t % 2) + 1))
                for b in range(S // P):
                    blk = slice(b * P, (b + 1) * P)
                    nc.tensor.transpose(rise_bank[:, blk], rise_t[:, blk], ident[:])
                rise = keep.tile([P, S], F32, name="rise%d" % t, align_bytes=64)
                fall = keep.tile([P, S], F32, name="fall%d" % t, align_bytes=64)
                nc.scalar.copy(rise[:], rise_bank[:])
                nc.scalar.activation(fall[:], rise_bank[:], COPY, scale=-1.0)
                nc.vector.tensor_tensor(pages[t][:].indirect(n3_l[:]), h_t[:], rise[:], ALU.add)
                nc.vector.tensor_tensor(pages[t][:].indirect(n4_l[:]), other[:], fall[:], ALU.add)
            nc.sync.dma_start(out_rows[t], pages[t][:])
